import numpy as np, ml_dtypes
CORES = [35,38,43,46]
N = 4
import mx_ref
NC, WB = 512, 1
D = 2 * WB + 1
BF = ml_dtypes.bfloat16
def setup_inputs(rng):
    def f(*shape):
        return mx_ref.flush((rng.standard_normal(shape, dtype=np.float32) * np.exp2(rng.integers(-2, 3, shape[:-1] + (1,)))).astype(BF))
    return {"w": f(N, 128, 512), "x": f(N, 128, 4 * NC)}
def setup_inputs_blocks(rng):
    d = setup_inputs(rng)
    for k in ("w", "x"): d[k] = mx_ref.spread(d[k], rng, 4)
    return d
def setup_inputs_wide(rng):
    d = setup_inputs(rng)
    for k in ("w", "x"): d[k] = mx_ref.flush((d[k].astype(np.float32) * np.exp2(rng.integers(-8, 9, (N, 1, 1))).astype(np.float32)).astype(BF))
    return d
def setup_inputs_zeros(rng):
    d = setup_inputs(rng); v = d["x"].reshape(N, 128, -1, 4).copy()
    v[np.broadcast_to((rng.random((N, 1, v.shape[2], 1)) < 0.33), v.shape)] = 0
    d["x"] = v.reshape(d["x"].shape)
    return d
def reference(w, x):
    QX = [mx_ref.quantize(x[j]) for j in range(N)]
    y = np.zeros((N, 128, D * NC), np.float32)
    for r in range(N):
        qw = mx_ref.quantize(w[r])
        for i in range(D):
            y[r][:, NC * i:NC * i + NC] = mx_ref.matmul(qw, QX[(r + i - WB) % N])
    return {"y": y}

@@ -1,0 +1,135 @@
+from concourse.bass import DstId, RemoteDMATransfer
+from concourse.mybir import dt, ActivationFunctionType
+
+NC = 512
+CHUNKS = [256, 256]
+NCH = len(CHUNKS)
+OFF = [sum(CHUNKS[:i]) for i in range(NCH + 1)]
+
+SCRATCH = {
+    "xs": ("sbuf", [128, 4 * NC], "bfloat16"),
+    "ws": ("sbuf", [128, 512], "bfloat16"),
+    "qx": ("sbuf", [128, NC], "float8_e4m3fn_x4"),
+    "sx": ("sbuf", [128, NC], "uint8"),
+    "qw": ("sbuf", [128, 128], "float8_e4m3fn_x4"),
+    "sw": ("sbuf", [128, 128], "uint8"),
+    "qa": ("sbuf", [128, NC], "float8_e4m3fn_x4"),
+    "sa": ("sbuf", [128, NC], "uint8"),
+    "qb": ("sbuf", [128, NC], "float8_e4m3fn_x4"),
+    "sb": ("sbuf", [128, NC], "uint8"),
+    "ps": ("psum", [128, 512 * (1 + 2 * NCH)], "float32"),
+    "yb": ("sbuf", [128, 3 * NC], "float32"),
+}
+SEMAPHORES = (["lw", "qws", "sent", "mo", "co", "st_sync", "st_scal"]
+              + ["lx%d" % c for c in range(NCH)] + ["qs%d" % c for c in range(NCH)]
+              + ["%s%s%d" % (k, s, c) for k in ("arr", "mm", "cp") for s in "ab" for c in range(NCH)])
+
+
+def _bits(m):
+    return [e for e in range(m.bit_length()) if (m >> e) & 1]
+
+
+def _pow2_floor(n):
+    return 1 << (n.bit_length() - 1)
+
+
+def rank_program(g, core, T, topo):
+    rank = T.rank_of(core)
+    if rank is None:
+        return
+    n = len(T.cores)
+    S = T.sem
+    prev, nxt = T.cores[(rank - 1) % n], T.cores[(rank + 1) % n]
+
+    ldq = [g.sync, g.scalar]
+    for c in range(NCH):
+        a, b = 4 * OFF[c], 4 * OFF[c + 1]
+        ldq[c % 2].dma_start(T.xs[:, a:b], T.x[:, a:b]).then_inc(S["lx%d" % c], 16)
+    ldq[NCH % 2].dma_start(T.ws[:], T.w[:]).then_inc(S.lw, 16)
+
+    for c in range(NCH):
+        a, b = OFF[c], OFF[c + 1]
+        g.vector.wait_ge(S["lx%d" % c], 16)
+        g.vector.quantize_mx(T.qx[:, a:b], T.sx[:, a:b], T.xs[:, 4 * a:4 * b]).then_inc(S["qs%d" % c], 1)
+    g.vector.wait_ge(S.lw, 16)
+    g.vector.quantize_mx(T.qw[:], T.sw[:], T.ws[:]).then_inc(S.qws, 1)
+
+    dests = [(nxt, "a"), (prev, "b")]
+    allowed = {d: _bits(topo.mask(core, d)) for d, _ in dests}
+    every = sorted(set(e for d, _ in dests for e in allowed[d]))
+    share = _pow2_floor(len(every) // len(dests))
+    taken, masks, width = set(), {}, {}
+    for d, _ in sorted(dests, key=lambda t: len(allowed[t[0]])):
+        free = [e for e in allowed[d] if e not in taken]
+        k = min(share, _pow2_floor(len(free)))
+        masks[d] = sum(1 << e for e in free[:k])
+        width[d] = k
+        taken.update(free[:k])
+    sent = 0
+    for c in range(NCH):
+        a, b = OFF[c], OFF[c + 1]
+        g.wait_ge(S["qs%d" % c], 1)
+        for plane in (False, True):
+            trs = []
+            for d, side in dests:
+                rid, pid, _ = topo.addr(d)
+                if plane:
+                    src, dst = T.sx[:, a:b], T["s" + side][:, a:b]
+                else:
+                    src, dst = T.qx[:, a:b].bitcast(dt.uint8), T["q" + side][:, a:b].bitcast(dt.uint8)
+                trs.append(RemoteDMATransfer(dst_ids=[DstId(rid=rid, pnc=pid)], dma_engine_mask=masks[d],
+                                             remote_sem=S["arr%s%d" % (side, c)], src=src, dst=dst))
+                sent += width[d]
+            g.remote_dma_fused(trs, local_sem=S.sent)
+
+    g.tensor.wait_ge(S.qws, 1)
+    for c in range(NCH):
+        g.tensor.wait_ge(S["qs%d" % c], 1)
+    g.tensor.matmul_mx(T.ps[:, 0:NC], T.qw[:], T.sw[:], T.qx[:], T.sx[:], True, True).then_inc(S.mo, 1)
+    g.scalar.wait_ge(S.mo, 1)
+    g.scalar.activation(T.yb[:, NC:2 * NC], T.ps[:, 0:NC], ActivationFunctionType.Copy).then_inc(S.co, 1)
+    g.sync.wait_ge(S.co, 1)
+    g.sync.dma_start(T.y[:, NC:2 * NC], T.yb[:, NC:2 * NC]).then_inc(S.st_sync, 16)
+    n_sync, n_scal = 16, 0
+
+    def sender_width(s):
+        r = T.rank_of(s)
+        ds = [T.cores[(r + 1) % n], T.cores[(r - 1) % n]]
+        al = {d: _bits(topo.mask(s, d)) for d in ds}
+        sh = _pow2_floor(len(set(e for d in ds for e in al[d])) // len(ds))
+        tk = set()
+        for d in sorted(ds, key=lambda t: len(al[t])):
+            fr = [e for e in al[d] if e not in tk]
+            k = min(sh, _pow2_floor(len(fr)))
+            if d == core:
+                return k
+            tk.update(fr[:k])
+
+    sides = [("a", prev, 0), ("b", nxt, 2)]
+    sides.sort(key=lambda t: topo.chip(t[1]) != topo.chip(core))
+    for c in range(NCH):
+        a, b = OFF[c], OFF[c + 1]
+        for i, (side, s, blk) in enumerate(sides):
+            bank = 512 * (1 + c * 2 + i)
+            pv = T.ps[:, bank:bank + (b - a)]
+            yv = T.yb[:, blk * NC + a:blk * NC + b]
+            mm, cp = S["mm%s%d" % (side, c)], S["cp%s%d" % (side, c)]
+            g.tensor.wait_ge(S["arr%s%d" % (side, c)], 2 * sender_width(s))
+            g.tensor.matmul_mx(pv, T.qw[:], T.sw[:], T["q" + side][:, a:b], T["s" + side][:, a:b],
+                               True, True).then_inc(mm, 1)
+            if i == 0:
+                g.vector.wait_ge(mm, 1)
+                g.vector.tensor_copy(yv, pv).then_inc(cp, 1)
+                g.sync.wait_ge(cp, 1)
+                g.sync.dma_start(T.y[:, blk * NC + a:blk * NC + b], yv).then_inc(S.st_sync, 16)
+                n_sync += 16
+            else:
+                g.scalar.wait_ge(mm, 1)
+                g.scalar.activation(yv, pv, ActivationFunctionType.Copy).then_inc(cp, 1)
+                g.scalar.wait_ge(cp, 1)
+                g.scalar.dma_start(T.y[:, blk * NC + a:blk * NC + b], yv).then_inc(S.st_scal, 16)
+                n_scal += 16
+
+    g.wait_ge(S.sent, sent)
+    g.sync.wait_ge(S.st_sync, n_sync)
+    g.scalar.wait_ge(S.st_scal, n_scal)

@@ -2,7 +2,7 @@ from concourse.bass import DstId, RemoteDMATransfer
 from concourse.mybir import dt, ActivationFunctionType
 
 NC = 512
-CHUNKS = [256, 256]
+CHUNKS = [128, 256, 128]
 NCH = len(CHUNKS)
 OFF = [sum(CHUNKS[:i]) for i in range(NCH + 1)]
 
@@ -20,7 +20,7 @@ SCRATCH = {
     "ps": ("psum", [128, 512 * (1 + 2 * NCH)], "float32"),
     "yb": ("sbuf", [128, 3 * NC], "float32"),
 }
-SEMAPHORES = (["lw", "qws", "sent", "mo", "co", "st_sync", "st_scal"]
+SEMAPHORES = (["lw", "qws", "sent", "mo", "co", "st_sync", "st_scal", "pla", "plb"]
               + ["lx%d" % c for c in range(NCH)] + ["qs%d" % c for c in range(NCH)]
               + ["%s%s%d" % (k, s, c) for k in ("arr", "mm", "cp") for s in "ab" for c in range(NCH)])
 
@@ -57,30 +57,38 @@ def rank_program(g, core, T, topo):
     dests = [(nxt, "a"), (prev, "b")]
     allowed = {d: _bits(topo.mask(core, d)) for d, _ in dests}
     every = sorted(set(e for d, _ in dests for e in allowed[d]))
-    share = _pow2_floor(len(every) // len(dests))
+    half = len(every) // len(dests)
     taken, masks, width = set(), {}, {}
     for d, _ in sorted(dests, key=lambda t: len(allowed[t[0]])):
         free = [e for e in allowed[d] if e not in taken]
-        k = min(share, _pow2_floor(len(free)))
+        k = _pow2_floor(min(half, len(free)))
         masks[d] = sum(1 << e for e in free[:k])
         width[d] = k
         taken.update(free[:k])
-    sent = 0
-    for c in range(NCH):
-        a, b = OFF[c], OFF[c + 1]
+    sent = [0]
+
+    def send(piece):
+        trs = []
+        for d, side in dests:
+            rid, pid, _ = topo.addr(d)
+            if piece is None:
+                src, dst, sem = T.sx[:], T["s" + side][:], S["pl" + side]
+            else:
+                a, b = OFF[piece], OFF[piece + 1]
+                src, dst = T.qx[:, a:b].bitcast(dt.uint8), T["q" + side][:, a:b].bitcast(dt.uint8)
+                sem = S["arr%s%d" % (side, piece)]
+            trs.append(RemoteDMATransfer(dst_ids=[DstId(rid=rid, pnc=pid)], dma_engine_mask=masks[d],
+                                         remote_sem=sem, src=src, dst=dst))
+            sent[0] += width[d]
+        g.remote_dma_fused(trs, local_sem=S.sent)
+
+    g.wait_ge(S.qs0, 1)
+    send(0)
+    for c in range(1, NCH):
         g.wait_ge(S["qs%d" % c], 1)
-        for plane in (False, True):
-            trs = []
-            for d, side in dests:
-                rid, pid, _ = topo.addr(d)
-                if plane:
-                    src, dst = T.sx[:, a:b], T["s" + side][:, a:b]
-                else:
-                    src, dst = T.qx[:, a:b].bitcast(dt.uint8), T["q" + side][:, a:b].bitcast(dt.uint8)
-                trs.append(RemoteDMATransfer(dst_ids=[DstId(rid=rid, pnc=pid)], dma_engine_mask=masks[d],
-                                             remote_sem=S["arr%s%d" % (side, c)], src=src, dst=dst))
-                sent += width[d]
-            g.remote_dma_fused(trs, local_sem=S.sent)
+    send(None)
+    for c in range(1, NCH):
+        send(c)
 
     g.tensor.wait_ge(S.qws, 1)
     for c in range(NCH):
@@ -92,19 +100,6 @@ def rank_program(g, core, T, topo):
     g.sync.dma_start(T.y[:, NC:2 * NC], T.yb[:, NC:2 * NC]).then_inc(S.st_sync, 16)
     n_sync, n_scal = 16, 0
 
-    def sender_width(s):
-        r = T.rank_of(s)
-        ds = [T.cores[(r + 1) % n], T.cores[(r - 1) % n]]
-        al = {d: _bits(topo.mask(s, d)) for d in ds}
-        sh = _pow2_floor(len(set(e for d in ds for e in al[d])) // len(ds))
-        tk = set()
-        for d in sorted(ds, key=lambda t: len(al[t])):
-            fr = [e for e in al[d] if e not in tk]
-            k = min(sh, _pow2_floor(len(fr)))
-            if d == core:
-                return k
-            tk.update(fr[:k])
-
     sides = [("a", prev, 0), ("b", nxt, 2)]
     sides.sort(key=lambda t: topo.chip(t[1]) != topo.chip(core))
     for c in range(NCH):
@@ -114,7 +109,9 @@ def rank_program(g, core, T, topo):
             pv = T.ps[:, bank:bank + (b - a)]
             yv = T.yb[:, blk * NC + a:blk * NC + b]
             mm, cp = S["mm%s%d" % (side, c)], S["cp%s%d" % (side, c)]
-            g.tensor.wait_ge(S["arr%s%d" % (side, c)], 2 * sender_width(s))
+            if c == 0:
+                g.tensor.wait_ge(S["pl" + side], width[s])
+            g.tensor.wait_ge(S["arr%s%d" % (side, c)], width[s])
             g.tensor.matmul_mx(pv, T.qw[:], T.sw[:], T["q" + side][:, a:b], T["s" + side][:, a:b],
                                True, True).then_inc(mm, 1)
             if i == 0:
@@ -130,6 +127,6 @@ def rank_program(g, core, T, topo):
                 g.scalar.dma_start(T.y[:, blk * NC + a:blk * NC + b], yv).then_inc(S.st_scal, 16)
                 n_scal += 16
 
-    g.wait_ge(S.sent, sent)
+    g.wait_ge(S.sent, sent[0])
     g.sync.wait_ge(S.st_sync, n_sync)
     g.scalar.wait_ge(S.st_scal, n_scal)

from concourse.bass import DstId, RemoteDMATransfer
from concourse.mybir import dt, ActivationFunctionType

NC = 512
CHUNKS = [128, 256, 128]
NCH = len(CHUNKS)
OFF = [sum(CHUNKS[:i]) for i in range(NCH + 1)]

SCRATCH = {
    "xs": ("sbuf", [128, 4 * NC], "bfloat16"),
    "ws": ("sbuf", [128, 512], "bfloat16"),
    "qx": ("sbuf", [128, NC], "float8_e4m3fn_x4"),
    "sx": ("sbuf", [128, NC], "uint8"),
    "qw": ("sbuf", [128, 128], "float8_e4m3fn_x4"),
    "sw": ("sbuf", [128, 128], "uint8"),
    "qa": ("sbuf", [128, NC], "float8_e4m3fn_x4"),
    "sa": ("sbuf", [128, NC], "uint8"),
    "qb": ("sbuf", [128, NC], "float8_e4m3fn_x4"),
    "sb": ("sbuf", [128, NC], "uint8"),
    "ps": ("psum", [128, 512 * (1 + 2 * NCH)], "float32"),
    "yb": ("sbuf", [128, 3 * NC], "float32"),
}
SEMAPHORES = (["lw", "qws", "sent", "mo", "co", "st_sync", "st_scal", "pla", "plb"]
              + ["lx%d" % c for c in range(NCH)] + ["qs%d" % c for c in range(NCH)]
              + ["%s%s%d" % (k, s, c) for k in ("arr", "mm", "cp") for s in "ab" for c in range(NCH)])


def _bits(m):
    return [e for e in range(m.bit_length()) if (m >> e) & 1]


def _pow2_floor(n):
    return 1 << (n.bit_length() - 1)


def rank_program(g, core, T, topo):
    rank = T.rank_of(core)
    if rank is None:
        return
    n = len(T.cores)
    S = T.sem
    prev, nxt = T.cores[(rank - 1) % n], T.cores[(rank + 1) % n]

    ldq = [g.sync, g.scalar]
    for c in range(NCH):
        a, b = 4 * OFF[c], 4 * OFF[c + 1]
        ldq[c % 2].dma_start(T.xs[:, a:b], T.x[:, a:b]).then_inc(S["lx%d" % c], 16)
    ldq[NCH % 2].dma_start(T.ws[:], T.w[:]).then_inc(S.lw, 16)

    for c in range(NCH):
        a, b = OFF[c], OFF[c + 1]
        g.vector.wait_ge(S["lx%d" % c], 16)
        g.vector.quantize_mx(T.qx[:, a:b], T.sx[:, a:b], T.xs[:, 4 * a:4 * b]).then_inc(S["qs%d" % c], 1)
    g.vector.wait_ge(S.lw, 16)
    g.vector.quantize_mx(T.qw[:], T.sw[:], T.ws[:]).then_inc(S.qws, 1)

    dests = [(nxt, "a"), (prev, "b")]
    allowed = {d: _bits(topo.mask(core, d)) for d, _ in dests}
    every = sorted(set(e for d, _ in dests for e in allowed[d]))
    half = len(every) // len(dests)
    taken, masks, width = set(), {}, {}
    for d, _ in sorted(dests, key=lambda t: len(allowed[t[0]])):
        free = [e for e in allowed[d] if e not in taken]
        k = _pow2_floor(min(half, len(free)))
        masks[d] = sum(1 << e for e in free[:k])
        width[d] = k
        taken.update(free[:k])
    sent = [0]

    def send(piece):
        trs = []
        for d, side in dests:
            rid, pid, _ = topo.addr(d)
            if piece is None:
                src, dst, sem = T.sx[:], T["s" + side][:], S["pl" + side]
            else:
                a, b = OFF[piece], OFF[piece + 1]
                src, dst = T.qx[:, a:b].bitcast(dt.uint8), T["q" + side][:, a:b].bitcast(dt.uint8)
                sem = S["arr%s%d" % (side, piece)]
            trs.append(RemoteDMATransfer(dst_ids=[DstId(rid=rid, pnc=pid)], dma_engine_mask=masks[d],
                                         remote_sem=sem, src=src, dst=dst))
            sent[0] += width[d]
        g.remote_dma_fused(trs, local_sem=S.sent)

    g.wait_ge(S.qs0, 1)
    send(0)
    for c in range(1, NCH):
        g.wait_ge(S["qs%d" % c], 1)
    send(None)
    for c in range(1, NCH):
        send(c)

    g.tensor.wait_ge(S.qws, 1)
    for c in range(NCH):
        g.tensor.wait_ge(S["qs%d" % c], 1)
    g.tensor.matmul_mx(T.ps[:, 0:NC], T.qw[:], T.sw[:], T.qx[:], T.sx[:], True, True).then_inc(S.mo, 1)
    g.scalar.wait_ge(S.mo, 1)
    g.scalar.activation(T.yb[:, NC:2 * NC], T.ps[:, 0:NC], ActivationFunctionType.Copy).then_inc(S.co, 1)
    g.sync.wait_ge(S.co, 1)
    g.sync.dma_start(T.y[:, NC:2 * NC], T.yb[:, NC:2 * NC]).then_inc(S.st_sync, 16)
    n_sync, n_scal = 16, 0

    sides = [("a", prev, 0), ("b", nxt, 2)]
    sides.sort(key=lambda t: topo.chip(t[1]) != topo.chip(core))
    for c in range(NCH):
        a, b = OFF[c], OFF[c + 1]
        for i, (side, s, blk) in enumerate(sides):
            bank = 512 * (1 + c * 2 + i)
            pv = T.ps[:, bank:bank + (b - a)]
            yv = T.yb[:, blk * NC + a:blk * NC + b]
            mm, cp = S["mm%s%d" % (side, c)], S["cp%s%d" % (side, c)]
            if c == 0:
                g.tensor.wait_ge(S["pl" + side], width[s])
            g.tensor.wait_ge(S["arr%s%d" % (side, c)], width[s])
            g.tensor.matmul_mx(pv, T.qw[:], T.sw[:], T["q" + side][:, a:b], T["s" + side][:, a:b],
                               True, True).then_inc(mm, 1)
            if i == 0:
                g.vector.wait_ge(mm, 1)
                g.vector.tensor_copy(yv, pv).then_inc(cp, 1)
                g.sync.wait_ge(cp, 1)
                g.sync.dma_start(T.y[:, blk * NC + a:blk * NC + b], yv).then_inc(S.st_sync, 16)
                n_sync += 16
            else:
                g.scalar.wait_ge(mm, 1)
                g.scalar.activation(yv, pv, ActivationFunctionType.Copy).then_inc(cp, 1)
                g.scalar.wait_ge(cp, 1)
                g.scalar.dma_start(T.y[:, blk * NC + a:blk * NC + b], yv).then_inc(S.st_scal, 16)
                n_scal += 16

    g.wait_ge(S.sent, sent[0])
    g.sync.wait_ge(S.st_sync, n_sync)
    g.scalar.wait_ge(S.st_scal, n_scal)
